import numpy as np
import ml_dtypes

BF16 = ml_dtypes.bfloat16


def bf(x):
    return np.asarray(x, np.float32).astype(BF16)


def f32(x):
    return np.asarray(x, np.float32)


def f64(x):
    return np.asarray(x).astype(np.float64)


def striped(idx):
    return np.tile(idx.reshape(-1, 16).T, (8, 1))


S, K, M, N, D, V = 1024, 256, 512, 256, 4, 64


def gelu_tanh(v):
    return 0.5 * v * (1.0 + np.tanh(np.sqrt(2.0 / np.pi) * (v + 0.044715 * v**3)))


def setup_inputs():
    return {"table": bf(np.random.standard_normal((S, K))), "w": bf(np.random.standard_normal((K, M)) / np.sqrt(K)), "b": f32(0.5 * np.random.standard_normal((M, 1))), "offs": striped(np.random.permutation(S)[:N])}


def reference(table, w, b, offs):
    idx = offs[:16].T.reshape(-1)
    x = f64(table)[idx].T
    y = f64(w).T @ x
    z = gelu_tanh(y + f64(b))
    return z.reshape(M, V, D).max(axis=2)

@@ -1,0 +1,77 @@
+import concourse.mybir as mybir
+from concourse.masks import make_identity
+
+BF16, F32, U16 = mybir.dt.bfloat16, mybir.dt.float32, mybir.dt.uint16
+
+P = 128
+S, K, M, N, D = 1024, 256, 512, 256, 4
+V = N // D
+S_BLOCKS, K_BLOCKS, M_BLOCKS = S // P, K // P, M // P
+PAIR = 2 * P
+
+FLOPS = 2 * K * M * N
+
+
+def tile_gather_matmul_kernel(tc, table, w, b, offs, out):
+    nc = tc.nc
+    with (
+        tc.tile_pool(name="held", bufs=1) as held,
+        tc.tile_pool(name="work", bufs=2) as work,
+        tc.psum_pool(name="flip", bufs=4) as flip,
+        tc.psum_pool(name="sums", bufs=4) as sums,
+    ):
+        offsets = held.tile([P, N // 16], U16, name="offsets")
+        nc.sync.dma_start(offsets[:], offs)
+
+        rows = [held.tile([P, K], BF16, name=f"rows{s}") for s in range(S_BLOCKS)]
+        for s in range(S_BLOCKS):
+            queue = nc.sync if s % 2 == 0 else nc.scalar
+            queue.dma_start(rows[s][:], table[s * P : (s + 1) * P, :])
+
+        identity = held.tile([P, P], BF16, name="identity")
+        make_identity(nc, identity[:])
+
+        weights = [held.tile([P, M], BF16, name=f"weights{k}") for k in range(K_BLOCKS)]
+        for k in range(K_BLOCKS):
+            nc.gpsimd.dma_start(weights[k][:], w[k * P : (k + 1) * P, :])
+        bias = held.tile([P, M_BLOCKS], F32, name="bias")
+        with nc.allow_non_contiguous_dma(reason="one bias value to a partition"):
+            nc.gpsimd.dma_start(bias[:], b.rearrange("(a p) o -> p (a o)", p=P))
+
+        window = [held.tile([P, S], BF16, name=f"window{k}") for k in range(K_BLOCKS)]
+        for s in range(0, S_BLOCKS, 2):
+            for k in range(K_BLOCKS):
+                turned = flip.tile([P, PAIR], BF16, name="turned")
+                for half in range(2):
+                    nc.tensor.transpose(
+                        turned[:, half * P : (half + 1) * P],
+                        rows[s + half][:, k * P : (k + 1) * P],
+                        identity[:],
+                    )
+                if k == 0:
+                    nc.vector.tensor_copy(window[k][:, s * P : s * P + PAIR], turned[:])
+                else:
+                    nc.scalar.copy(window[k][:, s * P : s * P + PAIR], turned[:])
+
+        for m in range(M_BLOCKS):
+            y = sums.tile([P, N], F32, name="y")
+            for k in range(K_BLOCKS):
+                nc.tensor.matmul(
+                    y[:],
+                    weights[k][:, m * P : (m + 1) * P],
+                    window[k][:].indirect(offsets[:]),
+                    start=(k == 0),
+                    stop=(k == K_BLOCKS - 1),
+                )
+            z = work.tile([P, N], F32, name="z")
+            nc.scalar.activation(
+                z[:], y[:], mybir.ActivationFunctionType.Gelu_apprx_tanh, bias=bias[:, m : m + 1]
+            )
+            pooled = work.tile([P, V], F32, name="pooled")
+            nc.vector.tensor_reduce(
+                pooled[:],
+                z[:].rearrange("p (v d) -> p v d", d=D),
+                axis=mybir.AxisListType.X,
+                op=mybir.AluOpType.max,
+            )
+            nc.sync.dma_start(out[m * P : (m + 1) * P, :], pooled[:])

@@ -33,10 +33,10 @@ def tile_gather_matmul_kernel(tc, table, w, b, offs, out):
 
         weights = [held.tile([P, M], BF16, name=f"weights{k}") for k in range(K_BLOCKS)]
         for k in range(K_BLOCKS):
-            nc.gpsimd.dma_start(weights[k][:], w[k * P : (k + 1) * P, :])
+            nc.scalar.dma_start(weights[k][:], w[k * P : (k + 1) * P, :])
         bias = held.tile([P, M_BLOCKS], F32, name="bias")
         with nc.allow_non_contiguous_dma(reason="one bias value to a partition"):
-            nc.gpsimd.dma_start(bias[:], b.rearrange("(a p) o -> p (a o)", p=P))
+            nc.sync.dma_start(bias[:], b.rearrange("(a p) o -> p (a o)", p=P))
 
         window = [held.tile([P, S], BF16, name=f"window{k}") for k in range(K_BLOCKS)]
         for s in range(0, S_BLOCKS, 2):
@@ -48,10 +48,7 @@ def tile_gather_matmul_kernel(tc, table, w, b, offs, out):
                         rows[s + half][:, k * P : (k + 1) * P],
                         identity[:],
                     )
-                if k == 0:
-                    nc.vector.tensor_copy(window[k][:, s * P : s * P + PAIR], turned[:])
-                else:
-                    nc.scalar.copy(window[k][:, s * P : s * P + PAIR], turned[:])
+                nc.vector.tensor_copy(window[k][:, s * P : s * P + PAIR], turned[:])
 
         for m in range(M_BLOCKS):
             y = sums.tile([P, N], F32, name="y")

@@ -6,7 +6,8 @@ BF16, F32, U16 = mybir.dt.bfloat16, mybir.dt.float32, mybir.dt.uint16
 P = 128
 S, K, M, N, D = 1024, 256, 512, 256, 4
 V = N // D
-S_BLOCKS, K_BLOCKS, M_BLOCKS = S // P, K // P, M // P
+S_BLOCKS, M_BLOCKS = S // P, M // P
+E = K // P
 PAIR = 2 * P
 
 FLOPS = 2 * K * M * N
@@ -28,37 +29,35 @@ def tile_gather_matmul_kernel(tc, table, w, b, offs, out):
             queue = nc.sync if s % 2 == 0 else nc.scalar
             queue.dma_start(rows[s][:], table[s * P : (s + 1) * P, :])
 
-        identity = held.tile([P, P], BF16, name="identity")
+        identity = held.tile([P, P], F32, name="identity")
         make_identity(nc, identity[:])
 
-        weights = [held.tile([P, M], BF16, name=f"weights{k}") for k in range(K_BLOCKS)]
-        for k in range(K_BLOCKS):
-            nc.scalar.dma_start(weights[k][:], w[k * P : (k + 1) * P, :])
+        weights = held.tile([P, E, M], BF16, name="weights")
+        nc.scalar.dma_start(weights[:], w.rearrange("(p e) m -> p e m", e=E))
         bias = held.tile([P, M_BLOCKS], F32, name="bias")
         with nc.allow_non_contiguous_dma(reason="one bias value to a partition"):
             nc.sync.dma_start(bias[:], b.rearrange("(a p) o -> p (a o)", p=P))
 
-        window = [held.tile([P, S], BF16, name=f"window{k}") for k in range(K_BLOCKS)]
+        window = [held.tile([P, S], BF16, name=f"window{e}") for e in range(E)]
         for s in range(0, S_BLOCKS, 2):
-            for k in range(K_BLOCKS):
-                turned = flip.tile([P, PAIR], BF16, name="turned")
-                for half in range(2):
-                    nc.tensor.transpose(
-                        turned[:, half * P : (half + 1) * P],
-                        rows[s + half][:, k * P : (k + 1) * P],
-                        identity[:],
-                    )
-                nc.vector.tensor_copy(window[k][:, s * P : s * P + PAIR], turned[:])
+            turned = flip.tile([P, PAIR], F32, name="turned")
+            for half in range(2):
+                nc.tensor.transpose(
+                    turned[:, half * P : (half + 1) * P], rows[s + half][:].bitcast(F32), identity[:]
+                )
+            parted = turned[:].bitcast(BF16).rearrange("p (n e) -> p n e", e=E)
+            for e in range(E):
+                nc.vector.tensor_copy(window[e][:, s * P : s * P + PAIR], parted[:, :, e])
 
         for m in range(M_BLOCKS):
             y = sums.tile([P, N], F32, name="y")
-            for k in range(K_BLOCKS):
+            for e in range(E):
                 nc.tensor.matmul(
                     y[:],
-                    weights[k][:, m * P : (m + 1) * P],
-                    window[k][:].indirect(offsets[:]),
-                    start=(k == 0),
-                    stop=(k == K_BLOCKS - 1),
+                    weights[:, e, m * P : (m + 1) * P],
+                    window[e][:].indirect(offsets[:]),
+                    start=(e == 0),
+                    stop=(e == E - 1),
                 )
             z = work.tile([P, N], F32, name="z")
             nc.scalar.activation(

@@ -6,9 +6,10 @@ BF16, F32, U16 = mybir.dt.bfloat16, mybir.dt.float32, mybir.dt.uint16
 P = 128
 S, K, M, N, D = 1024, 256, 512, 256, 4
 V = N // D
-S_BLOCKS, M_BLOCKS = S // P, M // P
-E = K // P
+S_BLOCKS, K_BLOCKS, M_BLOCKS = S // P, K // P, M // P
 PAIR = 2 * P
+
+WARM_UPS = 4
 
 FLOPS = 2 * K * M * N
 
@@ -29,35 +30,45 @@ def tile_gather_matmul_kernel(tc, table, w, b, offs, out):
             queue = nc.sync if s % 2 == 0 else nc.scalar
             queue.dma_start(rows[s][:], table[s * P : (s + 1) * P, :])
 
-        identity = held.tile([P, P], F32, name="identity")
+        zeros = held.tile([P, 4 * P], BF16, name="zeros")
+        nc.vector.memset(zeros[:], 0.0)
+        unused = sums.tile([P, 4 * P], F32, name="unused", tag="y")
+        for i in range(WARM_UPS):
+            nc.tensor.matmul(unused[:], zeros[:, 0:P], zeros[:], start=True, stop=True)
+
+        identity = held.tile([P, P], BF16, name="identity")
         make_identity(nc, identity[:])
 
-        weights = held.tile([P, E, M], BF16, name="weights")
-        nc.scalar.dma_start(weights[:], w.rearrange("(p e) m -> p e m", e=E))
+        weights = [held.tile([P, M], BF16, name=f"weights{k}") for k in range(K_BLOCKS)]
+        for k in range(K_BLOCKS):
+            nc.scalar.dma_start(weights[k][:], w[k * P : (k + 1) * P, :])
         bias = held.tile([P, M_BLOCKS], F32, name="bias")
         with nc.allow_non_contiguous_dma(reason="one bias value to a partition"):
             nc.sync.dma_start(bias[:], b.rearrange("(a p) o -> p (a o)", p=P))
 
-        window = [held.tile([P, S], BF16, name=f"window{e}") for e in range(E)]
+        window = [held.tile([P, S], BF16, name=f"window{k}") for k in range(K_BLOCKS)]
         for s in range(0, S_BLOCKS, 2):
-            turned = flip.tile([P, PAIR], F32, name="turned")
+            for k in range(K_BLOCKS):
+                turned = flip.tile([P, PAIR], BF16, name="turned")
+                for half in range(2):
+                    nc.tensor.transpose(
+                        turned[:, half * P : (half + 1) * P],
+                        rows[s + half][:, k * P : (k + 1) * P],
+                        identity[:],
+                    )
+                nc.vector.tensor_copy(window[k][:, s * P : s * P + PAIR], turned[:])
             for half in range(2):
-                nc.tensor.transpose(
-                    turned[:, half * P : (half + 1) * P], rows[s + half][:].bitcast(F32), identity[:]
-                )
-            parted = turned[:].bitcast(BF16).rearrange("p (n e) -> p n e", e=E)
-            for e in range(E):
-                nc.vector.tensor_copy(window[e][:, s * P : s * P + PAIR], parted[:, :, e])
+                nc.tensor.matmul(unused[:, 0:K], identity[:], rows[s + half][:], start=True, stop=True)
 
         for m in range(M_BLOCKS):
             y = sums.tile([P, N], F32, name="y")
-            for e in range(E):
+            for k in range(K_BLOCKS):
                 nc.tensor.matmul(
                     y[:],
-                    weights[:, e, m * P : (m + 1) * P],
-                    window[e][:].indirect(offsets[:]),
-                    start=(e == 0),
-                    stop=(e == E - 1),
+                    weights[k][:, m * P : (m + 1) * P],
+                    window[k][:].indirect(offsets[:]),
+                    start=(k == 0),
+                    stop=(k == K_BLOCKS - 1),
                 )
             z = work.tile([P, N], F32, name="z")
             nc.scalar.activation(

@@ -2,14 +2,14 @@ import concourse.mybir as mybir
 from concourse.masks import make_identity
 
 BF16, F32, U16 = mybir.dt.bfloat16, mybir.dt.float32, mybir.dt.uint16
+GELU = mybir.ActivationFunctionType.Gelu_apprx_tanh
 
 P = 128
 S, K, M, N, D = 1024, 256, 512, 256, 4
 V = N // D
 S_BLOCKS, K_BLOCKS, M_BLOCKS = S // P, K // P, M // P
 PAIR = 2 * P
-
-WARM_UPS = 4
+FLIP_BANKS = 8 - M_BLOCKS
 
 FLOPS = 2 * K * M * N
 
@@ -18,62 +18,57 @@ def tile_gather_matmul_kernel(tc, table, w, b, offs, out):
     nc = tc.nc
     with (
         tc.tile_pool(name="held", bufs=1) as held,
-        tc.tile_pool(name="work", bufs=2) as work,
-        tc.psum_pool(name="flip", bufs=4) as flip,
-        tc.psum_pool(name="sums", bufs=4) as sums,
+        tc.tile_pool(name="work", bufs=M_BLOCKS) as work,
+        tc.psum_pool(name="flip", bufs=FLIP_BANKS) as flip,
+        tc.psum_pool(name="sums", bufs=M_BLOCKS) as sums,
     ):
+        rows = [held.tile([P, K], BF16, name=f"rows{sb}") for sb in range(S_BLOCKS)]
+        for sb in range(S_BLOCKS):
+            queue = nc.sync if sb % 2 == 0 else nc.scalar
+            queue.dma_start(rows[sb][:], table[sb * P : (sb + 1) * P, :])
+
         offsets = held.tile([P, N // 16], U16, name="offsets")
         nc.sync.dma_start(offsets[:], offs)
-
-        rows = [held.tile([P, K], BF16, name=f"rows{s}") for s in range(S_BLOCKS)]
-        for s in range(S_BLOCKS):
-            queue = nc.sync if s % 2 == 0 else nc.scalar
-            queue.dma_start(rows[s][:], table[s * P : (s + 1) * P, :])
-
-        zeros = held.tile([P, 4 * P], BF16, name="zeros")
-        nc.vector.memset(zeros[:], 0.0)
-        unused = sums.tile([P, 4 * P], F32, name="unused", tag="y")
-        for i in range(WARM_UPS):
-            nc.tensor.matmul(unused[:], zeros[:, 0:P], zeros[:], start=True, stop=True)
 
         identity = held.tile([P, P], BF16, name="identity")
         make_identity(nc, identity[:])
 
-        weights = [held.tile([P, M], BF16, name=f"weights{k}") for k in range(K_BLOCKS)]
-        for k in range(K_BLOCKS):
-            nc.scalar.dma_start(weights[k][:], w[k * P : (k + 1) * P, :])
+        weights = [held.tile([P, M], BF16, name=f"weights{kb}") for kb in range(K_BLOCKS)]
+        for kb in range(K_BLOCKS):
+            nc.scalar.dma_start(weights[kb][:], w[kb * P : (kb + 1) * P, :])
+
         bias = held.tile([P, M_BLOCKS], F32, name="bias")
         with nc.allow_non_contiguous_dma(reason="one bias value to a partition"):
-            nc.sync.dma_start(bias[:], b.rearrange("(a p) o -> p (a o)", p=P))
+            nc.sync.dma_start(bias[:], b.rearrange("(mb p) o -> p (mb o)", p=P))
 
-        window = [held.tile([P, S], BF16, name=f"window{k}") for k in range(K_BLOCKS)]
-        for s in range(0, S_BLOCKS, 2):
-            for k in range(K_BLOCKS):
+        zero = held.tile([P, 1], F32, name="zero")
+        nc.vector.memset(zero[:], 0.0)
+        nc.scalar.activation(zero[:], zero[:], GELU)
+
+        window = [held.tile([P, S], BF16, name=f"window{kb}") for kb in range(K_BLOCKS)]
+        for sb in range(0, S_BLOCKS, 2):
+            for kb in range(K_BLOCKS):
                 turned = flip.tile([P, PAIR], BF16, name="turned")
                 for half in range(2):
                     nc.tensor.transpose(
                         turned[:, half * P : (half + 1) * P],
-                        rows[s + half][:, k * P : (k + 1) * P],
+                        rows[sb + half][:, kb * P : (kb + 1) * P],
                         identity[:],
                     )
-                nc.vector.tensor_copy(window[k][:, s * P : s * P + PAIR], turned[:])
-            for half in range(2):
-                nc.tensor.matmul(unused[:, 0:K], identity[:], rows[s + half][:], start=True, stop=True)
+                nc.vector.tensor_copy(window[kb][:, sb * P : sb * P + PAIR], turned[:])
 
-        for m in range(M_BLOCKS):
+        for mb in range(M_BLOCKS):
             y = sums.tile([P, N], F32, name="y")
-            for k in range(K_BLOCKS):
+            for kb in range(K_BLOCKS):
                 nc.tensor.matmul(
                     y[:],
-                    weights[k][:, m * P : (m + 1) * P],
-                    window[k][:].indirect(offsets[:]),
-                    start=(k == 0),
-                    stop=(k == K_BLOCKS - 1),
+                    weights[kb][:, mb * P : (mb + 1) * P],
+                    window[kb][:].indirect(offsets[:]),
+                    start=(kb == 0),
+                    stop=(kb == K_BLOCKS - 1),
                 )
             z = work.tile([P, N], F32, name="z")
-            nc.scalar.activation(
-                z[:], y[:], mybir.ActivationFunctionType.Gelu_apprx_tanh, bias=bias[:, m : m + 1]
-            )
+            nc.scalar.activation(z[:], y[:], GELU, bias=bias[:, mb : mb + 1])
             pooled = work.tile([P, V], F32, name="pooled")
             nc.vector.tensor_reduce(
                 pooled[:],
@@ -81,4 +76,4 @@ def tile_gather_matmul_kernel(tc, table, w, b, offs, out):
                 axis=mybir.AxisListType.X,
                 op=mybir.AluOpType.max,
             )
-            nc.sync.dma_start(out[m * P : (m + 1) * P, :], pooled[:])
+            nc.sync.dma_start(out[mb * P : (mb + 1) * P, :], pooled[:])

@@ -24,8 +24,7 @@ def tile_gather_matmul_kernel(tc, table, w, b, offs, out):
     ):
         rows = [held.tile([P, K], BF16, name=f"rows{sb}") for sb in range(S_BLOCKS)]
         for sb in range(S_BLOCKS):
-            queue = nc.sync if sb % 2 == 0 else nc.scalar
-            queue.dma_start(rows[sb][:], table[sb * P : (sb + 1) * P, :])
+            nc.sync.dma_start(rows[sb][:], table[sb * P : (sb + 1) * P, :])
 
         offsets = held.tile([P, N // 16], U16, name="offsets")
         nc.sync.dma_start(offsets[:], offs)
@@ -35,7 +34,7 @@ def tile_gather_matmul_kernel(tc, table, w, b, offs, out):
 
         weights = [held.tile([P, M], BF16, name=f"weights{kb}") for kb in range(K_BLOCKS)]
         for kb in range(K_BLOCKS):
-            nc.scalar.dma_start(weights[kb][:], w[kb * P : (kb + 1) * P, :])
+            nc.sync.dma_start(weights[kb][:], w[kb * P : (kb + 1) * P, :])
 
         bias = held.tile([P, M_BLOCKS], F32, name="bias")
         with nc.allow_non_contiguous_dma(reason="one bias value to a partition"):

@@ -9,7 +9,8 @@ S, K, M, N, D = 1024, 256, 512, 256, 4
 V = N // D
 S_BLOCKS, K_BLOCKS, M_BLOCKS = S // P, K // P, M // P
 PAIR = 2 * P
-FLIP_BANKS = 8 - M_BLOCKS
+HALF = S_BLOCKS // 2
+BANKS = 8
 
 FLOPS = 2 * K * M * N
 
@@ -19,8 +20,7 @@ def tile_gather_matmul_kernel(tc, table, w, b, offs, out):
     with (
         tc.tile_pool(name="held", bufs=1) as held,
         tc.tile_pool(name="work", bufs=M_BLOCKS) as work,
-        tc.psum_pool(name="flip", bufs=FLIP_BANKS) as flip,
-        tc.psum_pool(name="sums", bufs=M_BLOCKS) as sums,
+        tc.psum_pool(name="banks", bufs=BANKS) as banks,
     ):
         rows = [held.tile([P, K], BF16, name=f"rows{sb}") for sb in range(S_BLOCKS)]
         for sb in range(S_BLOCKS):
@@ -45,19 +45,23 @@ def tile_gather_matmul_kernel(tc, table, w, b, offs, out):
         nc.scalar.activation(zero[:], zero[:], GELU)
 
         window = [held.tile([P, S], BF16, name=f"window{kb}") for kb in range(K_BLOCKS)]
-        for sb in range(0, S_BLOCKS, 2):
+        for first in range(0, S_BLOCKS, HALF):
             for kb in range(K_BLOCKS):
-                turned = flip.tile([P, PAIR], BF16, name="turned")
-                for half in range(2):
-                    nc.tensor.transpose(
-                        turned[:, half * P : (half + 1) * P],
-                        rows[sb + half][:, kb * P : (kb + 1) * P],
-                        identity[:],
-                    )
-                nc.vector.tensor_copy(window[kb][:, sb * P : sb * P + PAIR], turned[:])
+                for sb in range(first, first + HALF, 2):
+                    turned = banks.tile([P, PAIR], BF16, name="turned", tag="bank")
+                    for odd in range(2):
+                        nc.tensor.transpose(
+                            turned[:, odd * P : (odd + 1) * P],
+                            rows[sb + odd][:, kb * P : (kb + 1) * P],
+                            identity[:],
+                        )
+                    if kb == 0:
+                        nc.vector.tensor_copy(window[kb][:, sb * P : sb * P + PAIR], turned[:])
+                    else:
+                        nc.scalar.copy(window[kb][:, sb * P : sb * P + PAIR], turned[:])
 
         for mb in range(M_BLOCKS):
-            y = sums.tile([P, N], F32, name="y")
+            y = banks.tile([P, N], F32, name="y", tag="bank")
             for kb in range(K_BLOCKS):
                 nc.tensor.matmul(
                     y[:],

@@ -9,7 +9,7 @@ S, K, M, N, D = 1024, 256, 512, 256, 4
 V = N // D
 S_BLOCKS, K_BLOCKS, M_BLOCKS = S // P, K // P, M // P
 PAIR = 2 * P
-HALF = S_BLOCKS // 2
+GROUPS = S // PAIR
 BANKS = 8
 
 FLOPS = 2 * K * M * N
@@ -22,9 +22,10 @@ def tile_gather_matmul_kernel(tc, table, w, b, offs, out):
         tc.tile_pool(name="work", bufs=M_BLOCKS) as work,
         tc.psum_pool(name="banks", bufs=BANKS) as banks,
     ):
-        rows = [held.tile([P, K], BF16, name=f"rows{sb}") for sb in range(S_BLOCKS)]
-        for sb in range(S_BLOCKS):
-            nc.sync.dma_start(rows[sb][:], table[sb * P : (sb + 1) * P, :])
+        rows = [held.tile([P, 2, K], BF16, name=f"rows{g}") for g in range(GROUPS)]
+        for g in range(GROUPS):
+            nodes = table[g * PAIR : (g + 1) * PAIR, :]
+            nc.sync.dma_start(rows[g][:], nodes.rearrange("(p r) k -> p r k", r=2))
 
         offsets = held.tile([P, N // 16], U16, name="offsets")
         nc.sync.dma_start(offsets[:], offs)
@@ -45,20 +46,21 @@ def tile_gather_matmul_kernel(tc, table, w, b, offs, out):
         nc.scalar.activation(zero[:], zero[:], GELU)
 
         window = [held.tile([P, S], BF16, name=f"window{kb}") for kb in range(K_BLOCKS)]
-        for first in range(0, S_BLOCKS, HALF):
+        for first in range(0, GROUPS, 2):
             for kb in range(K_BLOCKS):
-                for sb in range(first, first + HALF, 2):
-                    turned = banks.tile([P, PAIR], BF16, name="turned", tag="bank")
-                    for odd in range(2):
+                for g in (first, first + 1):
+                    turned = banks.tile([P, 2, P], BF16, name="turned", tag="bank")
+                    for r in range(2):
                         nc.tensor.transpose(
-                            turned[:, odd * P : (odd + 1) * P],
-                            rows[sb + odd][:, kb * P : (kb + 1) * P],
-                            identity[:],
+                            turned[:, r, :], rows[g][:, r, kb * P : (kb + 1) * P], identity[:]
                         )
+                    in_order = window[kb][:, g * PAIR : (g + 1) * PAIR].rearrange(
+                        "f (p r) -> f p r", r=2
+                    )
                     if kb == 0:
-                        nc.vector.tensor_copy(window[kb][:, sb * P : sb * P + PAIR], turned[:])
+                        nc.vector.tensor_copy(in_order, turned[:].rearrange("f r p -> f p r"))
                     else:
-                        nc.scalar.copy(window[kb][:, sb * P : sb * P + PAIR], turned[:])
+                        nc.scalar.copy(in_order, turned[:].rearrange("f r p -> f p r"))
 
         for mb in range(M_BLOCKS):
             y = banks.tile([P, N], F32, name="y", tag="bank")

@@ -11,6 +11,8 @@ S_BLOCKS, K_BLOCKS, M_BLOCKS = S // P, K // P, M // P
 PAIR = 2 * P
 GROUPS = S // PAIR
 BANKS = 8
+BANK_COLUMNS = 512
+WARMING_MATMULS = 3
 
 FLOPS = 2 * K * M * N
 
@@ -44,6 +46,12 @@ def tile_gather_matmul_kernel(tc, table, w, b, offs, out):
         zero = held.tile([P, 1], F32, name="zero")
         nc.vector.memset(zero[:], 0.0)
         nc.scalar.activation(zero[:], zero[:], GELU)
+
+        nothing = held.tile([P, BANK_COLUMNS], BF16, name="nothing")
+        nc.vector.memset(nothing[:], 0.0)
+        unread = banks.tile([P, BANK_COLUMNS], F32, name="unread", tag="bank")
+        for turn in range(WARMING_MATMULS):
+            nc.tensor.matmul(unread[:], nothing[:, 0:P], nothing[:], start=True, stop=True)
 
         window = [held.tile([P, S], BF16, name=f"window{kb}") for kb in range(K_BLOCKS)]
         for first in range(0, GROUPS, 2):

@@ -70,6 +70,15 @@ def tile_gather_matmul_kernel(tc, table, w, b, offs, out):
                     else:
                         nc.scalar.copy(in_order, turned[:].rearrange("f r p -> f p r"))
 
+        unread_too = banks.tile([P, BANK_COLUMNS], F32, name="unread_too", tag="bank")
+        nc.tensor.matmul(
+            unread_too[:],
+            nothing[:, 0:P],
+            rows[GROUPS - 1][:].rearrange("p r k -> p (r k)"),
+            start=True,
+            stop=True,
+        )
+
         for mb in range(M_BLOCKS):
             y = banks.tile([P, N], F32, name="y", tag="bank")
             for kb in range(K_BLOCKS):

import concourse.mybir as mybir
from concourse.masks import make_identity

BF16, F32, U16 = mybir.dt.bfloat16, mybir.dt.float32, mybir.dt.uint16
GELU = mybir.ActivationFunctionType.Gelu_apprx_tanh

P = 128
S, K, M, N, D = 1024, 256, 512, 256, 4
V = N // D
S_BLOCKS, K_BLOCKS, M_BLOCKS = S // P, K // P, M // P
PAIR = 2 * P
GROUPS = S // PAIR
BANKS = 8
BANK_COLUMNS = 512
WARMING_MATMULS = 3

FLOPS = 2 * K * M * N


def tile_gather_matmul_kernel(tc, table, w, b, offs, out):
    nc = tc.nc
    with (
        tc.tile_pool(name="held", bufs=1) as held,
        tc.tile_pool(name="work", bufs=M_BLOCKS) as work,
        tc.psum_pool(name="banks", bufs=BANKS) as banks,
    ):
        rows = [held.tile([P, 2, K], BF16, name=f"rows{g}") for g in range(GROUPS)]
        for g in range(GROUPS):
            nodes = table[g * PAIR : (g + 1) * PAIR, :]
            nc.sync.dma_start(rows[g][:], nodes.rearrange("(p r) k -> p r k", r=2))

        offsets = held.tile([P, N // 16], U16, name="offsets")
        nc.sync.dma_start(offsets[:], offs)

        identity = held.tile([P, P], BF16, name="identity")
        make_identity(nc, identity[:])

        weights = [held.tile([P, M], BF16, name=f"weights{kb}") for kb in range(K_BLOCKS)]
        for kb in range(K_BLOCKS):
            nc.sync.dma_start(weights[kb][:], w[kb * P : (kb + 1) * P, :])

        bias = held.tile([P, M_BLOCKS], F32, name="bias")
        with nc.allow_non_contiguous_dma(reason="one bias value to a partition"):
            nc.sync.dma_start(bias[:], b.rearrange("(mb p) o -> p (mb o)", p=P))

        zero = held.tile([P, 1], F32, name="zero")
        nc.vector.memset(zero[:], 0.0)
        nc.scalar.activation(zero[:], zero[:], GELU)

        nothing = held.tile([P, BANK_COLUMNS], BF16, name="nothing")
        nc.vector.memset(nothing[:], 0.0)
        unread = banks.tile([P, BANK_COLUMNS], F32, name="unread", tag="bank")
        for turn in range(WARMING_MATMULS):
            nc.tensor.matmul(unread[:], nothing[:, 0:P], nothing[:], start=True, stop=True)

        window = [held.tile([P, S], BF16, name=f"window{kb}") for kb in range(K_BLOCKS)]
        for first in range(0, GROUPS, 2):
            for kb in range(K_BLOCKS):
                for g in (first, first + 1):
                    turned = banks.tile([P, 2, P], BF16, name="turned", tag="bank")
                    for r in range(2):
                        nc.tensor.transpose(
                            turned[:, r, :], rows[g][:, r, kb * P : (kb + 1) * P], identity[:]
                        )
                    in_order = window[kb][:, g * PAIR : (g + 1) * PAIR].rearrange(
                        "f (p r) -> f p r", r=2
                    )
                    if kb == 0:
                        nc.vector.tensor_copy(in_order, turned[:].rearrange("f r p -> f p r"))
                    else:
                        nc.scalar.copy(in_order, turned[:].rearrange("f r p -> f p r"))

        unread_too = banks.tile([P, BANK_COLUMNS], F32, name="unread_too", tag="bank")
        nc.tensor.matmul(
            unread_too[:],
            nothing[:, 0:P],
            rows[GROUPS - 1][:].rearrange("p r k -> p (r k)"),
            start=True,
            stop=True,
        )

        for mb in range(M_BLOCKS):
            y = banks.tile([P, N], F32, name="y", tag="bank")
            for kb in range(K_BLOCKS):
                nc.tensor.matmul(
                    y[:],
                    weights[kb][:, mb * P : (mb + 1) * P],
                    window[kb][:].indirect(offsets[:]),
                    start=(kb == 0),
                    stop=(kb == K_BLOCKS - 1),
                )
            z = work.tile([P, N], F32, name="z")
            nc.scalar.activation(z[:], y[:], GELU, bias=bias[:, mb : mb + 1])
            pooled = work.tile([P, V], F32, name="pooled")
            nc.vector.tensor_reduce(
                pooled[:],
                z[:].rearrange("p (v d) -> p v d", d=D),
                axis=mybir.AxisListType.X,
                op=mybir.AluOpType.max,
            )
            nc.sync.dma_start(out[mb * P : (mb + 1) * P, :], pooled[:])
